import numpy as np
import ml_dtypes


def mxq(x, axis, fmt="e4m3"):
    dtype, down = {"e4m3": (ml_dtypes.float8_e4m3fn, 7), "e5m2": (ml_dtypes.float8_e5m2, 14)}[fmt]
    v = np.moveaxis(np.asarray(x, np.float32).astype(ml_dtypes.bfloat16).astype(np.float64), axis, -1)
    blocks = v.reshape(v.shape[:-1] + (-1, 32))
    amax = np.abs(blocks).max(-1, keepdims=True)
    byte = np.maximum(np.where(amax > 0, np.frexp(amax)[1] - 1 + 127, 0) - down, 1)
    scale = np.exp2(byte - 127.0)
    codes = (blocks / scale).astype(np.float32).astype(dtype).astype(np.float64)
    return np.moveaxis((codes * scale).reshape(v.shape), -1, axis)


WIDE = False


def mx_kscale(k):
    if not WIDE:
        return np.ones(k)
    levels = np.array([10, -10, 5, -5, 0])
    if k % 512:
        return np.exp2(np.random.permutation(np.resize(levels, k // 32))).repeat(32)
    a = np.empty((k // 512, 16))
    for p in range(k // 512):
        a[p, :8] = np.random.permutation(np.resize(levels, 8))
        for g in range(8):
            far = levels[np.abs(levels - a[p, g]) >= 10]
            a[p, g + 8] = far[np.random.randint(len(far))]
    return np.exp2(a.ravel()).repeat(32)


def f64(x):
    return np.asarray(x).astype(np.float64)


def striped8(idx):
    return np.asarray(idx).reshape(8, -1, 16).transpose(0, 2, 1).reshape(128, -1).astype(np.uint16)


def unstriped8(offs):
    return offs.reshape(8, 16, -1).transpose(0, 2, 1).reshape(8, -1).astype(np.int64)


def pick8(x, idx, run):
    r = np.arange(len(x))
    return x[r[:, None], idx[r % (8 * run) // run]]


E2M1 = np.array([0.0, 0.5, 1.0, 1.5, 2.0, 3.0, 4.0, 6.0, -0.0, -0.5, -1.0, -1.5, -2.0, -3.0, -4.0, -6.0])


def pack_weight(w, fmt):
    k, n = w.shape
    w = f64(np.asarray(w, np.float32).astype(ml_dtypes.bfloat16)).reshape(k // 32, 32, n)
    amax = np.abs(w).max(1)
    if fmt == "e4m3":
        byte = np.frexp(amax)[1] - 1 + 127 - 7
    else:
        mant, ex = np.frexp(amax / 6.0)
        byte = np.where(mant > 0.5, ex, ex - 1) + 127
    byte = np.clip(np.where(amax > 0, byte, 1), 1, 254)
    scaled = (w * np.exp2(127.0 - byte)[:, None, :]).reshape(k, n).astype(np.float32)
    by_word = np.ascontiguousarray(scaled.reshape(k // 512, 128, 4, n).transpose(0, 1, 3, 2))
    if fmt == "e4m3":
        words = by_word.astype(ml_dtypes.float8_e4m3fn).view(np.uint8)
    else:
        c = by_word.astype(ml_dtypes.float4_e2m1fn).view(np.uint8) & 0xF
        words = (c[..., 0::2] | (c[..., 1::2] << 4)).reshape(k // 512, 128, 2 * n)
    return np.ascontiguousarray(words), np.ascontiguousarray(byte.astype(np.uint8).reshape(k // 512, 16, n))


def unpack_weight(words, scales, fmt):
    g, _, n = scales.shape
    words = np.ascontiguousarray(words).reshape(g, 128, n, -1)
    if fmt == "e4m3":
        vals = words.view(ml_dtypes.float8_e4m3fn).astype(np.float64)
    else:
        nib = np.empty((g, 128, n, 4), np.uint8)
        nib[..., 0::2] = words & 0xF
        nib[..., 1::2] = words >> 4
        vals = E2M1[nib]
    vals = vals * np.repeat(np.exp2(scales.astype(np.float64) - 127.0), 8, axis=1)[..., None]
    return vals.transpose(0, 1, 3, 2).reshape(g * 512, n)


D, E, T, Q, I, G = 512, 512, 1024, 128, 512, 64


def setup_inputs():
    n = np.random.standard_normal
    idx = np.stack([np.random.permutation(T)[:I] for _ in range(8)])
    fd = mx_kscale(D)
    fe = mx_kscale(E)
    keysp = pack_weight(n((D, T)) / fd[:, None], "e4m3")
    return {
        "query": (n((D, Q)) * 0.7 / np.sqrt(D) * fd[:, None]).astype(np.float32),
        "keys_words": keysp[0],
        "keys_scales": keysp[1],
        "gout": (n((E, Q)) * 1 / np.sqrt(E) * fe[:, None]).astype(np.float32),
        "vals": (n((E, T)) / fe[:, None]).astype(np.float32),
        "quota": (np.random.uniform(0.3, 2.0, (Q, G))).astype(np.float32),
        "dquery": (n((D, Q)) * 1.0 / np.sqrt(D) * fd[:, None]).astype(np.float32),
        "base": (0.5 * n((Q, T))).astype(np.float32),
        "offs": striped8(idx),
    }


def reference(query, keys_words, keys_scales, gout, vals, quota, dquery, base, offs):
    idx = unstriped8(offs)
    keysu = unpack_weight(keys_words, keys_scales, "e4m3")
    queryq = mxq(f64(query), 0, "e4m3")
    a = queryq.T @ keysu
    dqueryq = mxq(f64(dquery), 0, "e4m3")
    ta = dqueryq.T @ keysu
    p = np.exp(pick8(a, idx, 16))
    u1 = f64(quota) / p.reshape(Q, G, I // G).sum(axis=2)
    ur = np.repeat(u1, I // G, axis=1)
    goutq = mxq(f64(gout), 0, "e4m3")
    valsq = mxq(f64(vals), 0, "e4m3")
    c0 = goutq.T @ valsq
    dw = pick8(c0, idx, 16)
    dur = dw * p
    du1 = dur.reshape(Q, G, I // G).sum(axis=2)
    e1 = du1 * f64(quota) / np.square(p.reshape(Q, G, I // G).sum(axis=2)) * (-1.0)
    r1 = np.repeat(e1, I // G, axis=1)
    dp = dw * ur + r1
    xp = pick8(ta, idx, 16) * p
    xu1 = xp.reshape(Q, G, I // G).sum(axis=2) * f64(quota) / np.square(p.reshape(Q, G, I // G).sum(axis=2)) * (-1.0)
    xur = np.repeat(xu1, I // G, axis=1)
    xdur = xp * dw
    xdu1 = xdur.reshape(Q, G, I // G).sum(axis=2)
    xe1 = (xdu1 * f64(quota) - xp.reshape(Q, G, I // G).sum(axis=2) * p.reshape(Q, G, I // G).sum(axis=2) * 2.0 * du1 * f64(quota) / np.square(p.reshape(Q, G, I // G).sum(axis=2))) / np.square(p.reshape(Q, G, I // G).sum(axis=2)) * (-1.0)
    xr1 = np.repeat(xe1, I // G, axis=1)
    xdp = xur * dw + xr1
    xe2 = xdp * p + xp * dp
    xs2 = np.zeros((Q, T))
    xs2[np.arange(Q)[:, None], idx[np.arange(Q) % 128 // 16]] = xe2
    y = xs2 * 8.0 + f64(base)
    return y

@@ -1,0 +1,191 @@
+from contextlib import ExitStack
+
+import concourse.mybir as mybir
+
+D, E, T, Q, I, G = 512, 512, 1024, 128, 512, 64
+FLOPS = 2 * Q * T * (2 * D + E)
+
+F32 = mybir.dt.float32
+BF16 = mybir.dt.bfloat16
+I32 = mybir.dt.int32
+U32 = mybir.dt.uint32
+U16 = mybir.dt.uint16
+U8 = mybir.dt.uint8
+FP8X4 = mybir.dt.float8_e4m3fn_x4
+MULT = mybir.AluOpType.mult
+ADD = mybir.AluOpType.add
+SUB = mybir.AluOpType.subtract
+EXP = mybir.ActivationFunctionType.Exp
+AXIS_X = mybir.AxisListType.X
+
+P = 128
+PACK = 4
+BANK = 512
+GROUP = I // G
+VAL_COLS = 256
+HALF = I // 2
+OUT_COLS = 256
+
+
+def tile_attend_hvquota_heads_kernel(tc, query, keys_words, keys_scales, gout, vals, quota, dquery, base, offs, out):
+    nc = tc.nc
+    with ExitStack() as ctx:
+        sb = ctx.enter_context(tc.tile_pool(name="sb", bufs=1))
+        ps = ctx.enter_context(tc.psum_pool(name="ps", bufs=1))
+
+        def load_rows(name, src):
+            raw = sb.tile([P, PACK, src.shape[1]], F32, name=name + "_raw")
+            nc.sync.dma_start(out=raw[:], in_=src.rearrange("(p j) w -> p j w", j=PACK))
+            return raw
+
+        def interleave(copy, woven, raw, c0, c1):
+            copy(
+                out=woven[:, c0:c1, :].rearrange("p (c i) j -> p c j i", i=4),
+                in_=raw[:, :, c0:c1].rearrange("p j (c i) -> p c j i", i=4),
+            )
+
+        def woven_tile(name, width):
+            return sb.tile([P, width, PACK], BF16, name=name + "_woven", align_bytes=64)
+
+        def quantize(name, woven):
+            width = woven.shape[1]
+            codes = sb.tile([P, width], U32, name=name + "_codes", align_bytes=64)
+            scales = sb.tile([P, width], U8, name=name + "_scales", align_bytes=64)
+            nc.vector.quantize_mx(out=codes[:].bitcast(FP8X4), scales=scales[:], in_=woven[:].rearrange("p w j -> p (w j)"))
+            return codes, scales
+
+        def product(name, stationary, codes, scales):
+            acc = ps.tile([P, codes.shape[1]], F32, name=name)
+            nc.tensor.matmul_mx(
+                out=acc[:], lhsT=stationary[0][:].bitcast(FP8X4), lhsT_scale=stationary[1][:],
+                rhs=codes.bitcast(FP8X4), rhs_scale=scales, start=True, stop=True,
+            )
+            return acc
+
+        def by_group(ap):
+            return ap.rearrange("p (g j) -> p g j", j=GROUP)
+
+        def spread(ap):
+            return ap.unsqueeze(2).to_broadcast([P, ap.shape[1], GROUP])
+
+        vcopy, scopy = nc.vector.tensor_copy, nc.scalar.copy
+
+        warm = sb.tile([P, 2], F32)
+        nc.vector.memset(warm[:, 0:1], 0.0)
+        nc.scalar.activation(out=warm[:, 1:2], in_=warm[:, 0:1], func=EXP)
+        key_scales = sb.tile([P, T], U8, align_bytes=64)
+        nc.gpsimd.memset(key_scales[:].bitcast(I32), 0)
+        placed = sb.tile([P, T], F32)
+        nc.gpsimd.memset(placed[:], 0.0)
+
+        quota_sb = sb.tile([P, G], F32)
+        nc.sync.dma_start(out=quota_sb[:], in_=quota)
+        query_raw = load_rows("query", query)
+        for quad in range(4):
+            nc.sync.dma_start(
+                out=key_scales[32 * quad : 32 * quad + 4, :].bitcast(I32),
+                in_=keys_scales[0, 4 * quad : 4 * quad + 4, :].bitcast(I32),
+            )
+        key_codes = sb.tile([P, T], U32, align_bytes=64)
+        nc.sync.dma_start(out=key_codes[:].bitcast(I32), in_=keys_words[0].rearrange("p n t -> p (n t)").bitcast(I32))
+        dquery_raw = load_rows("dquery", dquery)
+        offsets = sb.tile([P, I // 16], U16)
+        nc.sync.dma_start(offsets[:], offs)
+        n_val = T // VAL_COLS
+        val_raw = []
+        for c in range(n_val):
+            if c == 1:
+                gout_raw = load_rows("gout", gout)
+            val_raw.append(load_rows("vals%d" % c, vals[:, c * VAL_COLS : (c + 1) * VAL_COLS]))
+        base_sb = sb.tile([P, T], F32)
+        nc.sync.dma_start(out=base_sb[:], in_=base)
+
+        quota8 = sb.tile([P, I], F32)
+        nc.gpsimd.tensor_scalar(by_group(quota8[:]), spread(quota_sb[:]), 8.0, 0.0, MULT, ADD)
+
+        query_woven = woven_tile("query", Q)
+        interleave(vcopy, query_woven, query_raw, 0, Q)
+        query_mx = quantize("query", query_woven)
+        a = sb.tile([P, T], F32)
+        for b in range(2):
+            cols = slice(b * BANK, (b + 1) * BANK)
+            acc = product("a_acc%d" % b, query_mx, key_codes[:, cols], key_scales[:, cols])
+            (scopy, vcopy)[b](out=a[:, cols], in_=acc[:])
+        p = sb.tile([P, I], F32)
+        nc.scalar.activation(out=p[:], in_=a[:].indirect(offsets[:]), func=EXP)
+
+        dquery_woven = woven_tile("dquery", Q)
+        interleave(vcopy, dquery_woven, dquery_raw, 0, Q)
+        dquery_mx = quantize("dquery", dquery_woven)
+        ta = sb.tile([P, T], F32)
+        for b in range(2):
+            cols = slice(b * BANK, (b + 1) * BANK)
+            acc = product("ta_acc%d" % b, dquery_mx, key_codes[:, cols], key_scales[:, cols])
+            scopy(out=ta[:, cols], in_=acc[:])
+
+        val_woven = [woven_tile("vals%d" % c, VAL_COLS) for c in range(n_val)]
+        val_mx = []
+        interleave(vcopy, val_woven[0], val_raw[0], 0, VAL_COLS)
+        val_mx.append(quantize("vals0", val_woven[0]))
+
+        p_sum = sb.tile([P, G], F32)
+        nc.vector.tensor_reduce(out=p_sum[:], in_=by_group(p[:]), axis=AXIS_X, op=ADD)
+        p_inv = sb.tile([P, G], F32)
+        nc.vector.reciprocal(out=p_inv[:], in_=p_sum[:])
+        share = sb.tile([P, I], F32)
+        nc.vector.tensor_tensor(by_group(share[:]), by_group(p[:]), spread(p_inv[:]), MULT)
+
+        interleave(scopy, val_woven[1], val_raw[1], 0, VAL_COLS)
+        gout_woven = woven_tile("gout", Q)
+        interleave(vcopy, gout_woven, gout_raw, 0, Q)
+        gout_mx = quantize("gout", gout_woven)
+
+        tq = sb.tile([P, I], F32)
+        nc.vector.tensor_tensor(tq[:], ta[:].indirect(offsets[:]), quota8[:], MULT)
+        val_mx.append(quantize("vals1", val_woven[1]))
+        tq_share = sb.tile([P, I], F32)
+        nc.vector.tensor_tensor(tq_share[:], tq[:], share[:], MULT)
+        interleave(scopy, val_woven[2], val_raw[2], 0, VAL_COLS)
+        tq_mean = sb.tile([P, G], F32)
+        nc.vector.tensor_reduce(out=tq_mean[:], in_=by_group(tq_share[:]), axis=AXIS_X, op=ADD)
+        val_mx.append(quantize("vals2", val_woven[2]))
+        interleave(scopy, val_woven[3], val_raw[3], 0, VAL_COLS)
+        tq_dev = sb.tile([P, I], F32)
+        nc.vector.tensor_tensor(by_group(tq_dev[:]), by_group(tq[:]), spread(tq_mean[:]), SUB)
+        val_mx.append(quantize("vals3", val_woven[3]))
+
+        c0 = sb.tile([P, T], F32)
+        for c in range(n_val):
+            acc = product("c0_acc%d" % c, gout_mx, val_mx[c][0][:], val_mx[c][1][:])
+            scopy(out=c0[:, c * VAL_COLS : (c + 1) * VAL_COLS], in_=acc[:])
+
+        halves = [slice(h * HALF, (h + 1) * HALF) for h in range(2)]
+        lists = [offsets[:, h * HALF // 16 : (h + 1) * HALF // 16] for h in range(2)]
+        terms = [sb.tile([P, 2, HALF], F32, name="terms%d" % h) for h in range(2)]
+        sums = [sb.tile([P, 2, G // 2], F32, name="sums%d" % h) for h in range(2)]
+        shift = [sb.tile([P, HALF], F32, name="shift%d" % h) for h in range(2)]
+        shift2 = [sb.tile([P, HALF], F32, name="shift2_%d" % h) for h in range(2)]
+        shift3 = [sb.tile([P, HALF], F32, name="shift3_%d" % h) for h in range(2)]
+        for h in range(2):
+            nc.vector.tensor_tensor(terms[h][:, 0, :], c0[:].indirect(lists[h]), share[:, halves[h]], MULT)
+        for h in range(2):
+            nc.vector.tensor_tensor(terms[h][:, 1, :], terms[h][:, 0, :], tq_dev[:, halves[h]], MULT)
+        for h in range(2):
+            nc.vector.tensor_reduce(
+                out=sums[h][:].rearrange("p k g -> p (k g)"), in_=by_group(terms[h][:].rearrange("p k i -> p (k i)")),
+                axis=AXIS_X, op=ADD,
+            )
+        for h in range(2):
+            nc.vector.tensor_tensor(by_group(shift[h][:]), by_group(tq_dev[:, halves[h]]), spread(sums[h][:, 0, :]), MULT)
+        for h in range(2):
+            nc.vector.tensor_tensor(by_group(shift2[h][:]), by_group(shift[h][:]), spread(sums[h][:, 1, :]), ADD)
+        for h in range(2):
+            nc.vector.scalar_tensor_tensor(shift3[h][:], shift2[h][:], -1.0, share[:, halves[h]], MULT, MULT)
+        for h in range(2):
+            nc.vector.tensor_tensor(placed[:].indirect(lists[h]), terms[h][:, 1, :], shift3[h][:], ADD)
+
+        for c in range(T // OUT_COLS):
+            cols = slice(c * OUT_COLS, (c + 1) * OUT_COLS)
+            result = sb.tile([P, OUT_COLS], F32, name="result%d" % c)
+            nc.vector.tensor_tensor(result[:], placed[:, cols], base_sb[:, cols], ADD)
+            (nc.sync, nc.scalar)[c % 2].dma_start(out=out[:, cols], in_=result[:])

@@ -16,6 +16,7 @@ MULT = mybir.AluOpType.mult
 ADD = mybir.AluOpType.add
 SUB = mybir.AluOpType.subtract
 EXP = mybir.ActivationFunctionType.Exp
+COPY = mybir.ActivationFunctionType.Copy
 AXIS_X = mybir.AxisListType.X
 
 P = 128
@@ -31,10 +32,11 @@ def tile_attend_hvquota_heads_kernel(tc, query, keys_words, keys_scales, gout, v
     nc = tc.nc
     with ExitStack() as ctx:
         sb = ctx.enter_context(tc.tile_pool(name="sb", bufs=1))
+        over = ctx.enter_context(tc.tile_pool(name="over", bufs=1))
         ps = ctx.enter_context(tc.psum_pool(name="ps", bufs=1))
 
         def load_rows(name, src):
-            raw = sb.tile([P, PACK, src.shape[1]], F32, name=name + "_raw")
+            raw = sb.tile([P, PACK, src.shape[1]], F32, name=name + "_raw", tag=name + "_raw", align_bytes=64)
             nc.sync.dma_start(out=raw[:], in_=src.rearrange("(p j) w -> p j w", j=PACK))
             return raw
 
@@ -44,18 +46,18 @@ def tile_attend_hvquota_heads_kernel(tc, query, keys_words, keys_scales, gout, v
                 in_=raw[:, :, c0:c1].rearrange("p j (c i) -> p c j i", i=4),
             )
 
-        def woven_tile(name, width):
-            return sb.tile([P, width, PACK], BF16, name=name + "_woven", align_bytes=64)
+        def woven_tile(name, width, tag=""):
+            return sb.tile([P, width, PACK], BF16, name=name + "_woven", tag=tag or name + "_woven", align_bytes=64)
 
         def quantize(name, woven):
             width = woven.shape[1]
-            codes = sb.tile([P, width], U32, name=name + "_codes", align_bytes=64)
+            codes = sb.tile([P, width], U32, name=name + "_codes", tag=name + "_codes", align_bytes=64)
             scales = sb.tile([P, width], U8, name=name + "_scales", align_bytes=64)
             nc.vector.quantize_mx(out=codes[:].bitcast(FP8X4), scales=scales[:], in_=woven[:].rearrange("p w j -> p (w j)"))
             return codes, scales
 
         def product(name, stationary, codes, scales):
-            acc = ps.tile([P, codes.shape[1]], F32, name=name)
+            acc = ps.tile([P, codes.shape[1]], F32, name=name, tag=name)
             nc.tensor.matmul_mx(
                 out=acc[:], lhsT=stationary[0][:].bitcast(FP8X4), lhsT_scale=stationary[1][:],
                 rhs=codes.bitcast(FP8X4), rhs_scale=scales, start=True, stop=True,
@@ -86,101 +88,107 @@ def tile_attend_hvquota_heads_kernel(tc, query, keys_words, keys_scales, gout, v
                 out=key_scales[32 * quad : 32 * quad + 4, :].bitcast(I32),
                 in_=keys_scales[0, 4 * quad : 4 * quad + 4, :].bitcast(I32),
             )
+        key_words = keys_words[0].rearrange("p n t -> p (n t)").bitcast(I32)
         key_codes = sb.tile([P, T], U32, align_bytes=64)
-        nc.sync.dma_start(out=key_codes[:].bitcast(I32), in_=keys_words[0].rearrange("p n t -> p (n t)").bitcast(I32))
-        dquery_raw = load_rows("dquery", dquery)
-        offsets = sb.tile([P, I // 16], U16)
-        nc.sync.dma_start(offsets[:], offs)
+        nc.sync.dma_start(out=key_codes[:].bitcast(I32), in_=key_words)
         n_val = T // VAL_COLS
         val_raw = []
         for c in range(n_val):
             if c == 1:
+                dquery_raw = load_rows("dquery", dquery)
+                offsets = sb.tile([P, I // 16], U16)
+                nc.sync.dma_start(offsets[:], offs)
                 gout_raw = load_rows("gout", gout)
             val_raw.append(load_rows("vals%d" % c, vals[:, c * VAL_COLS : (c + 1) * VAL_COLS]))
         base_sb = sb.tile([P, T], F32)
         nc.sync.dma_start(out=base_sb[:], in_=base)
 
         quota8 = sb.tile([P, I], F32)
-        nc.gpsimd.tensor_scalar(by_group(quota8[:]), spread(quota_sb[:]), 8.0, 0.0, MULT, ADD)
+        nc.scalar.activation(out=by_group(quota8[:]), in_=spread(quota_sb[:]), func=COPY, scale=8.0)
 
         query_woven = woven_tile("query", Q)
         interleave(vcopy, query_woven, query_raw, 0, Q)
         query_mx = quantize("query", query_woven)
-        a = sb.tile([P, T], F32)
-        for b in range(2):
-            cols = slice(b * BANK, (b + 1) * BANK)
-            acc = product("a_acc%d" % b, query_mx, key_codes[:, cols], key_scales[:, cols])
-            (scopy, vcopy)[b](out=a[:, cols], in_=acc[:])
-        p = sb.tile([P, I], F32)
-        nc.scalar.activation(out=p[:], in_=a[:].indirect(offsets[:]), func=EXP)
+        halves = [slice(h * HALF, (h + 1) * HALF) for h in range(2)]
+        lists = [offsets[:, h * HALF // 16 : (h + 1) * HALF // 16] for h in range(2)]
+        a = over.tile([P, T], F32, offset=4032, align_bytes=64)
+        for b in range(n_val):
+            cols = slice(b * VAL_COLS, (b + 1) * VAL_COLS)
+            acc = product("bank%d" % b, query_mx, key_codes[:, cols], key_scales[:, cols])
+            scopy(out=a[:, cols], in_=acc[:])
+        p = [sb.tile([P, HALF], F32, name="p%d" % h) for h in range(2)]
+        for h in range(2):
+            nc.scalar.activation(out=p[h][:], in_=a[:].indirect(lists[h]), func=EXP)
 
-        dquery_woven = woven_tile("dquery", Q)
-        interleave(vcopy, dquery_woven, dquery_raw, 0, Q)
-        dquery_mx = quantize("dquery", dquery_woven)
-        ta = sb.tile([P, T], F32)
-        for b in range(2):
-            cols = slice(b * BANK, (b + 1) * BANK)
-            acc = product("ta_acc%d" % b, dquery_mx, key_codes[:, cols], key_scales[:, cols])
-            scopy(out=ta[:, cols], in_=acc[:])
-
-        val_woven = [woven_tile("vals%d" % c, VAL_COLS) for c in range(n_val)]
+        val_woven = [
+            woven_tile("vals0", VAL_COLS),
+            woven_tile("vals1", VAL_COLS),
+            over.tile([P, VAL_COLS, PACK], BF16, name="vals2_woven", offset=4096, align_bytes=64),
+            woven_tile("vals3", VAL_COLS, "vals2_raw"),
+        ]
         val_mx = []
         interleave(vcopy, val_woven[0], val_raw[0], 0, VAL_COLS)
         val_mx.append(quantize("vals0", val_woven[0]))
 
-        p_sum = sb.tile([P, G], F32)
-        nc.vector.tensor_reduce(out=p_sum[:], in_=by_group(p[:]), axis=AXIS_X, op=ADD)
-        p_inv = sb.tile([P, G], F32)
-        nc.vector.reciprocal(out=p_inv[:], in_=p_sum[:])
-        share = sb.tile([P, I], F32)
-        nc.vector.tensor_tensor(by_group(share[:]), by_group(p[:]), spread(p_inv[:]), MULT)
+        dquery_woven = woven_tile("dquery", Q)
+        interleave(vcopy, dquery_woven, dquery_raw, 0, Q)
+        dquery_mx = quantize("dquery", dquery_woven)
+        ta = over.tile([P, T], F32, offset=0, align_bytes=64)
+        for b in range(2):
+            cols = slice(b * BANK, (b + 1) * BANK)
+            acc = product("bank%d" % (4 + b), dquery_mx, key_codes[:, cols], key_scales[:, cols])
+            scopy(out=ta[:, cols], in_=acc[:])
 
-        interleave(scopy, val_woven[1], val_raw[1], 0, VAL_COLS)
         gout_woven = woven_tile("gout", Q)
         interleave(vcopy, gout_woven, gout_raw, 0, Q)
         gout_mx = quantize("gout", gout_woven)
 
-        tq = sb.tile([P, I], F32)
-        nc.vector.tensor_tensor(tq[:], ta[:].indirect(offsets[:]), quota8[:], MULT)
-        val_mx.append(quantize("vals1", val_woven[1]))
-        tq_share = sb.tile([P, I], F32)
-        nc.vector.tensor_tensor(tq_share[:], tq[:], share[:], MULT)
-        interleave(scopy, val_woven[2], val_raw[2], 0, VAL_COLS)
-        tq_mean = sb.tile([P, G], F32)
-        nc.vector.tensor_reduce(out=tq_mean[:], in_=by_group(tq_share[:]), axis=AXIS_X, op=ADD)
-        val_mx.append(quantize("vals2", val_woven[2]))
-        interleave(scopy, val_woven[3], val_raw[3], 0, VAL_COLS)
-        tq_dev = sb.tile([P, I], F32)
-        nc.vector.tensor_tensor(by_group(tq_dev[:]), by_group(tq[:]), spread(tq_mean[:]), SUB)
-        val_mx.append(quantize("vals3", val_woven[3]))
-
-        c0 = sb.tile([P, T], F32)
+        c0 = over.tile([P, T], F32, offset=6144, align_bytes=64)
+        for c in range(1, n_val):
+            interleave(vcopy if c == 1 else scopy, val_woven[c], val_raw[c], 0, VAL_COLS)
+            val_mx.append(quantize("vals%d" % c, val_woven[c]))
         for c in range(n_val):
-            acc = product("c0_acc%d" % c, gout_mx, val_mx[c][0][:], val_mx[c][1][:])
+            acc = product("bank%d" % ((6 + c) % 8), gout_mx, val_mx[c][0][:], val_mx[c][1][:])
             scopy(out=c0[:, c * VAL_COLS : (c + 1) * VAL_COLS], in_=acc[:])
 
-        halves = [slice(h * HALF, (h + 1) * HALF) for h in range(2)]
-        lists = [offsets[:, h * HALF // 16 : (h + 1) * HALF // 16] for h in range(2)]
+        def half_tiles(name, width):
+            return [sb.tile([P, width], F32, name="%s%d" % (name, h)) for h in range(2)]
+
+        p_sum, p_inv, tq_mean = (half_tiles(n, G // 2) for n in ("p_sum", "p_inv", "tq_mean"))
+        share, tq, tq_share, tq_dev = (half_tiles(n, HALF) for n in ("share", "tq", "tq_share", "tq_dev"))
+        for h in range(2):
+            nc.vector.tensor_reduce(out=p_sum[h][:], in_=by_group(p[h][:]), axis=AXIS_X, op=ADD)
+            nc.vector.reciprocal(out=p_inv[h][:], in_=p_sum[h][:])
+            nc.vector.tensor_tensor(by_group(share[h][:]), by_group(p[h][:]), spread(p_inv[h][:]), MULT)
+        for h in range(2):
+            nc.vector.tensor_tensor(tq[h][:], ta[:].indirect(lists[h]), quota8[:, halves[h]], MULT)
+        for h in range(2):
+            nc.vector.tensor_tensor(tq_share[h][:], tq[h][:], share[h][:], MULT)
+        for h in range(2):
+            nc.vector.tensor_reduce(out=tq_mean[h][:], in_=by_group(tq_share[h][:]), axis=AXIS_X, op=ADD)
+        for h in range(2):
+            nc.vector.tensor_tensor(by_group(tq_dev[h][:]), by_group(tq[h][:]), spread(tq_mean[h][:]), SUB)
+
         terms = [sb.tile([P, 2, HALF], F32, name="terms%d" % h) for h in range(2)]
         sums = [sb.tile([P, 2, G // 2], F32, name="sums%d" % h) for h in range(2)]
         shift = [sb.tile([P, HALF], F32, name="shift%d" % h) for h in range(2)]
         shift2 = [sb.tile([P, HALF], F32, name="shift2_%d" % h) for h in range(2)]
         shift3 = [sb.tile([P, HALF], F32, name="shift3_%d" % h) for h in range(2)]
         for h in range(2):
-            nc.vector.tensor_tensor(terms[h][:, 0, :], c0[:].indirect(lists[h]), share[:, halves[h]], MULT)
+            nc.vector.tensor_tensor(terms[h][:, 0, :], c0[:].indirect(lists[h]), share[h][:], MULT)
         for h in range(2):
-            nc.vector.tensor_tensor(terms[h][:, 1, :], terms[h][:, 0, :], tq_dev[:, halves[h]], MULT)
+            nc.vector.tensor_tensor(terms[h][:, 1, :], terms[h][:, 0, :], tq_dev[h][:], MULT)
         for h in range(2):
             nc.vector.tensor_reduce(
                 out=sums[h][:].rearrange("p k g -> p (k g)"), in_=by_group(terms[h][:].rearrange("p k i -> p (k i)")),
                 axis=AXIS_X, op=ADD,
             )
         for h in range(2):
-            nc.vector.tensor_tensor(by_group(shift[h][:]), by_group(tq_dev[:, halves[h]]), spread(sums[h][:, 0, :]), MULT)
+            nc.vector.tensor_tensor(by_group(shift[h][:]), by_group(tq_dev[h][:]), spread(sums[h][:, 0, :]), MULT)
         for h in range(2):
             nc.vector.tensor_tensor(by_group(shift2[h][:]), by_group(shift[h][:]), spread(sums[h][:, 1, :]), ADD)
         for h in range(2):
-            nc.vector.scalar_tensor_tensor(shift3[h][:], shift2[h][:], -1.0, share[:, halves[h]], MULT, MULT)
+            nc.vector.scalar_tensor_tensor(shift3[h][:], shift2[h][:], -1.0, share[h][:], MULT, MULT)
         for h in range(2):
             nc.vector.tensor_tensor(placed[:].indirect(lists[h]), terms[h][:, 1, :], shift3[h][:], ADD)
 

@@ -23,7 +23,9 @@ P = 128
 PACK = 4
 BANK = 512
 GROUP = I // G
-VAL_COLS = 256
+A_COLS = 256
+VAL_COLS = (256, 256, 256, 128, 128)
+VECTOR_PIECES = 2
 HALF = I // 2
 OUT_COLS = 256
 
@@ -72,9 +74,6 @@ def tile_attend_hvquota_heads_kernel(tc, query, keys_words, keys_scales, gout, v
 
         vcopy, scopy = nc.vector.tensor_copy, nc.scalar.copy
 
-        warm = sb.tile([P, 2], F32)
-        nc.vector.memset(warm[:, 0:1], 0.0)
-        nc.scalar.activation(out=warm[:, 1:2], in_=warm[:, 0:1], func=EXP)
         key_scales = sb.tile([P, T], U8, align_bytes=64)
         nc.gpsimd.memset(key_scales[:].bitcast(I32), 0)
         placed = sb.tile([P, T], F32)
@@ -91,7 +90,8 @@ def tile_attend_hvquota_heads_kernel(tc, query, keys_words, keys_scales, gout, v
         key_words = keys_words[0].rearrange("p n t -> p (n t)").bitcast(I32)
         key_codes = sb.tile([P, T], U32, align_bytes=64)
         nc.sync.dma_start(out=key_codes[:].bitcast(I32), in_=key_words)
-        n_val = T // VAL_COLS
+        n_val = len(VAL_COLS)
+        val_cols = [slice(sum(VAL_COLS[:c]), sum(VAL_COLS[: c + 1])) for c in range(n_val)]
         val_raw = []
         for c in range(n_val):
             if c == 1:
@@ -99,7 +99,7 @@ def tile_attend_hvquota_heads_kernel(tc, query, keys_words, keys_scales, gout, v
                 offsets = sb.tile([P, I // 16], U16)
                 nc.sync.dma_start(offsets[:], offs)
                 gout_raw = load_rows("gout", gout)
-            val_raw.append(load_rows("vals%d" % c, vals[:, c * VAL_COLS : (c + 1) * VAL_COLS]))
+            val_raw.append(load_rows("vals%d" % c, vals[:, val_cols[c]]))
         base_sb = sb.tile([P, T], F32)
         nc.sync.dma_start(out=base_sb[:], in_=base)
 
@@ -112,8 +112,8 @@ def tile_attend_hvquota_heads_kernel(tc, query, keys_words, keys_scales, gout, v
         halves = [slice(h * HALF, (h + 1) * HALF) for h in range(2)]
         lists = [offsets[:, h * HALF // 16 : (h + 1) * HALF // 16] for h in range(2)]
         a = over.tile([P, T], F32, offset=4032, align_bytes=64)
-        for b in range(n_val):
-            cols = slice(b * VAL_COLS, (b + 1) * VAL_COLS)
+        for b in range(T // A_COLS):
+            cols = slice(b * A_COLS, (b + 1) * A_COLS)
             acc = product("bank%d" % b, query_mx, key_codes[:, cols], key_scales[:, cols])
             scopy(out=a[:, cols], in_=acc[:])
         p = [sb.tile([P, HALF], F32, name="p%d" % h) for h in range(2)]
@@ -121,13 +121,14 @@ def tile_attend_hvquota_heads_kernel(tc, query, keys_words, keys_scales, gout, v
             nc.scalar.activation(out=p[h][:], in_=a[:].indirect(lists[h]), func=EXP)
 
         val_woven = [
-            woven_tile("vals0", VAL_COLS),
-            woven_tile("vals1", VAL_COLS),
-            over.tile([P, VAL_COLS, PACK], BF16, name="vals2_woven", offset=4096, align_bytes=64),
-            woven_tile("vals3", VAL_COLS, "vals2_raw"),
+            woven_tile("vals0", VAL_COLS[0]),
+            woven_tile("vals1", VAL_COLS[1]),
+            over.tile([P, VAL_COLS[2], PACK], BF16, name="vals2_woven", offset=4096, align_bytes=64),
+            woven_tile("vals3", VAL_COLS[3], "vals2_raw"),
+            woven_tile("vals4", VAL_COLS[4], "vals3_raw"),
         ]
         val_mx = []
-        interleave(vcopy, val_woven[0], val_raw[0], 0, VAL_COLS)
+        interleave(vcopy, val_woven[0], val_raw[0], 0, VAL_COLS[0])
         val_mx.append(quantize("vals0", val_woven[0]))
 
         dquery_woven = woven_tile("dquery", Q)
@@ -143,19 +144,22 @@ def tile_attend_hvquota_heads_kernel(tc, query, keys_words, keys_scales, gout, v
         interleave(vcopy, gout_woven, gout_raw, 0, Q)
         gout_mx = quantize("gout", gout_woven)
 
-        c0 = over.tile([P, T], F32, offset=6144, align_bytes=64)
+        c0 = sb.tile([P, T], F32, tag="vals4_raw", align_bytes=64)
         for c in range(1, n_val):
-            interleave(vcopy if c == 1 else scopy, val_woven[c], val_raw[c], 0, VAL_COLS)
+            interleave(vcopy if c < VECTOR_PIECES else scopy, val_woven[c], val_raw[c], 0, VAL_COLS[c])
             val_mx.append(quantize("vals%d" % c, val_woven[c]))
         for c in range(n_val):
             acc = product("bank%d" % ((6 + c) % 8), gout_mx, val_mx[c][0][:], val_mx[c][1][:])
-            scopy(out=c0[:, c * VAL_COLS : (c + 1) * VAL_COLS], in_=acc[:])
+            scopy(out=c0[:, val_cols[c]], in_=acc[:])
 
         def half_tiles(name, width):
             return [sb.tile([P, width], F32, name="%s%d" % (name, h)) for h in range(2)]
 
-        p_sum, p_inv, tq_mean = (half_tiles(n, G // 2) for n in ("p_sum", "p_inv", "tq_mean"))
-        share, tq, tq_share, tq_dev = (half_tiles(n, HALF) for n in ("share", "tq", "tq_share", "tq_dev"))
+        p_sum, p_inv = (half_tiles(n, G // 2) for n in ("p_sum", "p_inv"))
+        share, tq, tq_dev = (half_tiles(n, HALF) for n in ("share", "tq", "tq_dev"))
+        tq_share = [t[:] for t in half_tiles("tq_share", HALF)]
+        tq_means = sb.tile([P, G], F32, tag="vals3_raw", align_bytes=64)
+        tq_mean = [tq_means[:, h * G // 2 : (h + 1) * G // 2] for h in range(2)]
         for h in range(2):
             nc.vector.tensor_reduce(out=p_sum[h][:], in_=by_group(p[h][:]), axis=AXIS_X, op=ADD)
             nc.vector.reciprocal(out=p_inv[h][:], in_=p_sum[h][:])
@@ -163,11 +167,11 @@ def tile_attend_hvquota_heads_kernel(tc, query, keys_words, keys_scales, gout, v
         for h in range(2):
             nc.vector.tensor_tensor(tq[h][:], ta[:].indirect(lists[h]), quota8[:, halves[h]], MULT)
         for h in range(2):
-            nc.vector.tensor_tensor(tq_share[h][:], tq[h][:], share[h][:], MULT)
+            nc.vector.tensor_tensor(tq_share[h], tq[h][:], share[h][:], MULT)
         for h in range(2):
-            nc.vector.tensor_reduce(out=tq_mean[h][:], in_=by_group(tq_share[h][:]), axis=AXIS_X, op=ADD)
+            nc.vector.tensor_reduce(out=tq_mean[h], in_=by_group(tq_share[h]), axis=AXIS_X, op=ADD)
         for h in range(2):
-            nc.vector.tensor_tensor(by_group(tq_dev[h][:]), by_group(tq[h][:]), spread(tq_mean[h][:]), SUB)
+            nc.vector.tensor_tensor(by_group(tq_dev[h][:]), by_group(tq[h][:]), spread(tq_mean[h]), SUB)
 
         terms = [sb.tile([P, 2, HALF], F32, name="terms%d" % h) for h in range(2)]
         sums = [sb.tile([P, 2, G // 2], F32, name="sums%d" % h) for h in range(2)]

from contextlib import ExitStack

import concourse.mybir as mybir

D, E, T, Q, I, G = 512, 512, 1024, 128, 512, 64
FLOPS = 2 * Q * T * (2 * D + E)

F32 = mybir.dt.float32
BF16 = mybir.dt.bfloat16
I32 = mybir.dt.int32
U32 = mybir.dt.uint32
U16 = mybir.dt.uint16
U8 = mybir.dt.uint8
FP8X4 = mybir.dt.float8_e4m3fn_x4
MULT = mybir.AluOpType.mult
ADD = mybir.AluOpType.add
SUB = mybir.AluOpType.subtract
EXP = mybir.ActivationFunctionType.Exp
COPY = mybir.ActivationFunctionType.Copy
AXIS_X = mybir.AxisListType.X

P = 128
PACK = 4
BANK = 512
GROUP = I // G
A_COLS = 256
VAL_COLS = (256, 256, 256, 128, 128)
VECTOR_PIECES = 2
HALF = I // 2
OUT_COLS = 256


def tile_attend_hvquota_heads_kernel(tc, query, keys_words, keys_scales, gout, vals, quota, dquery, base, offs, out):
    nc = tc.nc
    with ExitStack() as ctx:
        sb = ctx.enter_context(tc.tile_pool(name="sb", bufs=1))
        over = ctx.enter_context(tc.tile_pool(name="over", bufs=1))
        ps = ctx.enter_context(tc.psum_pool(name="ps", bufs=1))

        def load_rows(name, src):
            raw = sb.tile([P, PACK, src.shape[1]], F32, name=name + "_raw", tag=name + "_raw", align_bytes=64)
            nc.sync.dma_start(out=raw[:], in_=src.rearrange("(p j) w -> p j w", j=PACK))
            return raw

        def interleave(copy, woven, raw, c0, c1):
            copy(
                out=woven[:, c0:c1, :].rearrange("p (c i) j -> p c j i", i=4),
                in_=raw[:, :, c0:c1].rearrange("p j (c i) -> p c j i", i=4),
            )

        def woven_tile(name, width, tag=""):
            return sb.tile([P, width, PACK], BF16, name=name + "_woven", tag=tag or name + "_woven", align_bytes=64)

        def quantize(name, woven):
            width = woven.shape[1]
            codes = sb.tile([P, width], U32, name=name + "_codes", tag=name + "_codes", align_bytes=64)
            scales = sb.tile([P, width], U8, name=name + "_scales", align_bytes=64)
            nc.vector.quantize_mx(out=codes[:].bitcast(FP8X4), scales=scales[:], in_=woven[:].rearrange("p w j -> p (w j)"))
            return codes, scales

        def product(name, stationary, codes, scales):
            acc = ps.tile([P, codes.shape[1]], F32, name=name, tag=name)
            nc.tensor.matmul_mx(
                out=acc[:], lhsT=stationary[0][:].bitcast(FP8X4), lhsT_scale=stationary[1][:],
                rhs=codes.bitcast(FP8X4), rhs_scale=scales, start=True, stop=True,
            )
            return acc

        def by_group(ap):
            return ap.rearrange("p (g j) -> p g j", j=GROUP)

        def spread(ap):
            return ap.unsqueeze(2).to_broadcast([P, ap.shape[1], GROUP])

        vcopy, scopy = nc.vector.tensor_copy, nc.scalar.copy

        key_scales = sb.tile([P, T], U8, align_bytes=64)
        nc.gpsimd.memset(key_scales[:].bitcast(I32), 0)
        placed = sb.tile([P, T], F32)
        nc.gpsimd.memset(placed[:], 0.0)

        quota_sb = sb.tile([P, G], F32)
        nc.sync.dma_start(out=quota_sb[:], in_=quota)
        query_raw = load_rows("query", query)
        for quad in range(4):
            nc.sync.dma_start(
                out=key_scales[32 * quad : 32 * quad + 4, :].bitcast(I32),
                in_=keys_scales[0, 4 * quad : 4 * quad + 4, :].bitcast(I32),
            )
        key_words = keys_words[0].rearrange("p n t -> p (n t)").bitcast(I32)
        key_codes = sb.tile([P, T], U32, align_bytes=64)
        nc.sync.dma_start(out=key_codes[:].bitcast(I32), in_=key_words)
        n_val = len(VAL_COLS)
        val_cols = [slice(sum(VAL_COLS[:c]), sum(VAL_COLS[: c + 1])) for c in range(n_val)]
        val_raw = []
        for c in range(n_val):
            if c == 1:
                dquery_raw = load_rows("dquery", dquery)
                offsets = sb.tile([P, I // 16], U16)
                nc.sync.dma_start(offsets[:], offs)
                gout_raw = load_rows("gout", gout)
            val_raw.append(load_rows("vals%d" % c, vals[:, val_cols[c]]))
        base_sb = sb.tile([P, T], F32)
        nc.sync.dma_start(out=base_sb[:], in_=base)

        quota8 = sb.tile([P, I], F32)
        nc.scalar.activation(out=by_group(quota8[:]), in_=spread(quota_sb[:]), func=COPY, scale=8.0)

        query_woven = woven_tile("query", Q)
        interleave(vcopy, query_woven, query_raw, 0, Q)
        query_mx = quantize("query", query_woven)
        halves = [slice(h * HALF, (h + 1) * HALF) for h in range(2)]
        lists = [offsets[:, h * HALF // 16 : (h + 1) * HALF // 16] for h in range(2)]
        a = over.tile([P, T], F32, offset=4032, align_bytes=64)
        for b in range(T // A_COLS):
            cols = slice(b * A_COLS, (b + 1) * A_COLS)
            acc = product("bank%d" % b, query_mx, key_codes[:, cols], key_scales[:, cols])
            scopy(out=a[:, cols], in_=acc[:])
        p = [sb.tile([P, HALF], F32, name="p%d" % h) for h in range(2)]
        for h in range(2):
            nc.scalar.activation(out=p[h][:], in_=a[:].indirect(lists[h]), func=EXP)

        val_woven = [
            woven_tile("vals0", VAL_COLS[0]),
            woven_tile("vals1", VAL_COLS[1]),
            over.tile([P, VAL_COLS[2], PACK], BF16, name="vals2_woven", offset=4096, align_bytes=64),
            woven_tile("vals3", VAL_COLS[3], "vals2_raw"),
            woven_tile("vals4", VAL_COLS[4], "vals3_raw"),
        ]
        val_mx = []
        interleave(vcopy, val_woven[0], val_raw[0], 0, VAL_COLS[0])
        val_mx.append(quantize("vals0", val_woven[0]))

        dquery_woven = woven_tile("dquery", Q)
        interleave(vcopy, dquery_woven, dquery_raw, 0, Q)
        dquery_mx = quantize("dquery", dquery_woven)
        ta = over.tile([P, T], F32, offset=0, align_bytes=64)
        for b in range(2):
            cols = slice(b * BANK, (b + 1) * BANK)
            acc = product("bank%d" % (4 + b), dquery_mx, key_codes[:, cols], key_scales[:, cols])
            scopy(out=ta[:, cols], in_=acc[:])

        gout_woven = woven_tile("gout", Q)
        interleave(vcopy, gout_woven, gout_raw, 0, Q)
        gout_mx = quantize("gout", gout_woven)

        c0 = sb.tile([P, T], F32, tag="vals4_raw", align_bytes=64)
        for c in range(1, n_val):
            interleave(vcopy if c < VECTOR_PIECES else scopy, val_woven[c], val_raw[c], 0, VAL_COLS[c])
            val_mx.append(quantize("vals%d" % c, val_woven[c]))
        for c in range(n_val):
            acc = product("bank%d" % ((6 + c) % 8), gout_mx, val_mx[c][0][:], val_mx[c][1][:])
            scopy(out=c0[:, val_cols[c]], in_=acc[:])

        def half_tiles(name, width):
            return [sb.tile([P, width], F32, name="%s%d" % (name, h)) for h in range(2)]

        p_sum, p_inv = (half_tiles(n, G // 2) for n in ("p_sum", "p_inv"))
        share, tq, tq_dev = (half_tiles(n, HALF) for n in ("share", "tq", "tq_dev"))
        tq_share = [t[:] for t in half_tiles("tq_share", HALF)]
        tq_means = sb.tile([P, G], F32, tag="vals3_raw", align_bytes=64)
        tq_mean = [tq_means[:, h * G // 2 : (h + 1) * G // 2] for h in range(2)]
        for h in range(2):
            nc.vector.tensor_reduce(out=p_sum[h][:], in_=by_group(p[h][:]), axis=AXIS_X, op=ADD)
            nc.vector.reciprocal(out=p_inv[h][:], in_=p_sum[h][:])
            nc.vector.tensor_tensor(by_group(share[h][:]), by_group(p[h][:]), spread(p_inv[h][:]), MULT)
        for h in range(2):
            nc.vector.tensor_tensor(tq[h][:], ta[:].indirect(lists[h]), quota8[:, halves[h]], MULT)
        for h in range(2):
            nc.vector.tensor_tensor(tq_share[h], tq[h][:], share[h][:], MULT)
        for h in range(2):
            nc.vector.tensor_reduce(out=tq_mean[h], in_=by_group(tq_share[h]), axis=AXIS_X, op=ADD)
        for h in range(2):
            nc.vector.tensor_tensor(by_group(tq_dev[h][:]), by_group(tq[h][:]), spread(tq_mean[h]), SUB)

        terms = [sb.tile([P, 2, HALF], F32, name="terms%d" % h) for h in range(2)]
        sums = [sb.tile([P, 2, G // 2], F32, name="sums%d" % h) for h in range(2)]
        shift = [sb.tile([P, HALF], F32, name="shift%d" % h) for h in range(2)]
        shift2 = [sb.tile([P, HALF], F32, name="shift2_%d" % h) for h in range(2)]
        shift3 = [sb.tile([P, HALF], F32, name="shift3_%d" % h) for h in range(2)]
        for h in range(2):
            nc.vector.tensor_tensor(terms[h][:, 0, :], c0[:].indirect(lists[h]), share[h][:], MULT)
        for h in range(2):
            nc.vector.tensor_tensor(terms[h][:, 1, :], terms[h][:, 0, :], tq_dev[h][:], MULT)
        for h in range(2):
            nc.vector.tensor_reduce(
                out=sums[h][:].rearrange("p k g -> p (k g)"), in_=by_group(terms[h][:].rearrange("p k i -> p (k i)")),
                axis=AXIS_X, op=ADD,
            )
        for h in range(2):
            nc.vector.tensor_tensor(by_group(shift[h][:]), by_group(tq_dev[h][:]), spread(sums[h][:, 0, :]), MULT)
        for h in range(2):
            nc.vector.tensor_tensor(by_group(shift2[h][:]), by_group(shift[h][:]), spread(sums[h][:, 1, :]), ADD)
        for h in range(2):
            nc.vector.scalar_tensor_tensor(shift3[h][:], shift2[h][:], -1.0, share[h][:], MULT, MULT)
        for h in range(2):
            nc.vector.tensor_tensor(placed[:].indirect(lists[h]), terms[h][:, 1, :], shift3[h][:], ADD)

        for c in range(T // OUT_COLS):
            cols = slice(c * OUT_COLS, (c + 1) * OUT_COLS)
            result = sb.tile([P, OUT_COLS], F32, name="result%d" % c)
            nc.vector.tensor_tensor(result[:], placed[:, cols], base_sb[:, cols], ADD)
            (nc.sync, nc.scalar)[c % 2].dma_start(out=out[:, cols], in_=result[:])
